import numpy as np, ml_dtypes
CORES = [31,71,111]
N = 3
def setup_inputs(rng):
    m = (rng.standard_normal((N, 128, 128), dtype=np.float32) / 11).astype(ml_dtypes.bfloat16)
    return {"m": m, "mt": m.transpose(0, 2, 1).copy()}
def setup_inputs_low(rng):
    d = setup_inputs(rng)
    for k in ("m", "mt"): d[k] = (d[k].astype(np.float32) * 0.125).astype(d[k].dtype)
    return d
def reference(m, mt):
    M = m.astype(np.float64); p = M[0]
    for r in range(1, N):
        p = p @ M[r]
    p = p.astype(ml_dtypes.bfloat16)
    return {"y": np.broadcast_to(p, (N, 128, 128))}

from concourse.bass import DstId, RemoteDMATransfer

SCRATCH = {
    "stage": ("dram", [128, 128], "bfloat16"),
    "A": ("sbuf", [128, 128], "bfloat16"),
    "B": ("sbuf", [128, 128], "bfloat16"),
    "C": ("sbuf", [128, 128], "bfloat16"),
    "S": ("sbuf", [128, 128], "bfloat16"),
    "O": ("sbuf", [128, 128], "bfloat16"),
    "p1": ("psum", [128, 512], "float32"),
    "p2": ("psum", [128, 512], "float32"),
}
SEMAPHORES = ["staged", "sent", "rdyA", "rdyB", "rdyC", "mm1", "cp1", "mm2", "cp2", "stored"]

NAMES = ["A", "B", "C"]
FIRST = {0: 2, 1: 0, 2: 1}


def _bits(mask):
    return sum(1 for e in range(16) if (mask >> e) & 1)


def rank_program(g, core, T, topo):
    rank = T.rank_of(core)
    if rank is None:
        return
    cores = T.cores
    n = len(cores)
    own = NAMES[rank]

    send_src = {0: T.mt, 1: T.m, 2: T.m}[rank]
    own_src = {0: T.mt, 1: T.mt, 2: T.m}[rank]
    g.sync.dma_start(T.stage[:], send_src[:]).then_inc(T.sem.staged, 16)
    g.sync.dma_start(T[own][:], own_src[:]).then_inc(T.sem["rdy" + own], 16)

    others = [FIRST[rank]] + [r for r in range(n) if r != rank and r != FIRST[rank]]
    mask = None
    ids = []
    for r in others:
        assert topo.may_write(core, cores[r])
        mk = topo.mask(core, cores[r])
        mask = mk if mask is None else (mask & mk)
        rid, pid, _se = topo.addr(cores[r])
        ids.append(DstId(rid=rid, pnc=pid))
    g.wait_ge(T.sem.staged, 16)
    g.remote_dma_fused(
        [RemoteDMATransfer(dst_ids=ids, dma_engine_mask=mask, remote_sem=T.sem["rdy" + own],
                           srcs=[T.stage[:]], dsts=[T[own][:] for _ in others], alu_op=0)],
        local_sem=T.sem.sent)

    need = {}
    for r in range(n):
        if r == rank:
            need[NAMES[r]] = 16
        else:
            mk = None
            for q in range(n):
                if q != r:
                    x = topo.mask(cores[r], cores[q])
                    mk = x if mk is None else (mk & x)
            need[NAMES[r]] = _bits(mk)

    def ready(name):
        g.tensor.wait_ge(T.sem["rdy" + name], need[name])

    if rank == 1:
        l1, r1 = "B", "C"
    else:
        l1, r1 = "B", "A"
    ready(l1)
    ready(r1)
    g.tensor.matmul(T.p1[:, 0:128], T[l1][:], T[r1][:], True, True).then_inc(T.sem.mm1, 1)
    g.vector.wait_ge(T.sem.mm1, 1)
    g.vector.tensor_copy(T.S[:], T.p1[:, 0:128]).then_inc(T.sem.cp1, 1)
    if rank == 1:
        ready("A")
        g.tensor.wait_ge(T.sem.cp1, 1)
        g.tensor.matmul(T.p2[:, 0:128], T.A[:], T.S[:], True, True).then_inc(T.sem.mm2, 1)
    else:
        ready("C")
        g.tensor.wait_ge(T.sem.cp1, 1)
        g.tensor.matmul(T.p2[:, 0:128], T.S[:], T.C[:], True, True).then_inc(T.sem.mm2, 1)
    g.vector.wait_ge(T.sem.mm2, 1)
    g.vector.tensor_copy(T.O[:], T.p2[:, 0:128]).then_inc(T.sem.cp2, 1)

    g.sync.wait_ge(T.sem.cp2, 1)
    g.sync.dma_start(T.y[:], T.O[:]).then_inc(T.sem.stored, 16)
    g.sync.wait_ge(T.sem.stored, 16)
    g.wait_ge(T.sem.sent, _bits(mask))
